import numpy as np
import ml_dtypes


def mxq(x, axis, fmt="e4m3"):
    dtype, down = {"e4m3": (ml_dtypes.float8_e4m3fn, 7), "e5m2": (ml_dtypes.float8_e5m2, 14)}[fmt]
    v = np.moveaxis(np.asarray(x, np.float32).astype(ml_dtypes.bfloat16).astype(np.float64), axis, -1)
    blocks = v.reshape(v.shape[:-1] + (-1, 32))
    amax = np.abs(blocks).max(-1, keepdims=True)
    byte = np.maximum(np.where(amax > 0, np.frexp(amax)[1] - 1 + 127, 0) - down, 1)
    scale = np.exp2(byte - 127.0)
    codes = (blocks / scale).astype(np.float32).astype(dtype).astype(np.float64)
    return np.moveaxis((codes * scale).reshape(v.shape), -1, axis)


WIDE = False


def mx_kscale(k):
    if not WIDE:
        return np.ones(k)
    levels = np.array([30, -30])
    if k % 512:
        return np.exp2(np.random.permutation(np.resize(levels, k // 32))).repeat(32)
    a = np.empty((k // 512, 16))
    for p in range(k // 512):
        a[p, :8] = np.random.permutation(np.resize(levels, 8))
        for g in range(8):
            far = levels[np.abs(levels - a[p, g]) >= 10]
            a[p, g + 8] = far[np.random.randint(len(far))]
    return np.exp2(a.ravel()).repeat(32)


def f64(x):
    return np.asarray(x).astype(np.float64)


E2M1 = np.array([0.0, 0.5, 1.0, 1.5, 2.0, 3.0, 4.0, 6.0, -0.0, -0.5, -1.0, -1.5, -2.0, -3.0, -4.0, -6.0])


def pack_weight(w, fmt):
    k, n = w.shape
    w = f64(np.asarray(w, np.float32).astype(ml_dtypes.bfloat16)).reshape(k // 32, 32, n)
    amax = np.abs(w).max(1)
    if fmt == "e4m3":
        byte = np.frexp(amax)[1] - 1 + 127 - 7
    else:
        mant, ex = np.frexp(amax / 6.0)
        byte = np.where(mant > 0.5, ex, ex - 1) + 127
    byte = np.clip(np.where(amax > 0, byte, 1), 1, 254)
    scaled = (w * np.exp2(127.0 - byte)[:, None, :]).reshape(k, n).astype(np.float32)
    by_word = np.ascontiguousarray(scaled.reshape(k // 512, 128, 4, n).transpose(0, 1, 3, 2))
    if fmt == "e4m3":
        words = by_word.astype(ml_dtypes.float8_e4m3fn).view(np.uint8)
    else:
        c = by_word.astype(ml_dtypes.float4_e2m1fn).view(np.uint8) & 0xF
        words = (c[..., 0::2] | (c[..., 1::2] << 4)).reshape(k // 512, 128, 2 * n)
    return np.ascontiguousarray(words), np.ascontiguousarray(byte.astype(np.uint8).reshape(k // 512, 16, n))


def unpack_weight(words, scales, fmt):
    g, _, n = scales.shape
    words = np.ascontiguousarray(words).reshape(g, 128, n, -1)
    if fmt == "e4m3":
        vals = words.view(ml_dtypes.float8_e4m3fn).astype(np.float64)
    else:
        nib = np.empty((g, 128, n, 4), np.uint8)
        nib[..., 0::2] = words & 0xF
        nib[..., 1::2] = words >> 4
        vals = E2M1[nib]
    vals = vals * np.repeat(np.exp2(scales.astype(np.float64) - 127.0), 8, axis=1)[..., None]
    return vals.transpose(0, 1, 3, 2).reshape(g * 512, n)


O, T, D, H = 1024, 1536, 768, 1024


def setup_inputs():
    n = np.random.standard_normal
    s = mx_kscale(T)[:, None]
    m = np.exp(0.5 * n((T, 1)))
    x = n((T, D)) * s
    p_x4 = pack_weight(x[:O], "e2m1")
    return {
        "x4_words": p_x4[0],
        "x4_scales": p_x4[1],
        "x8": (x[O:]).astype(np.float32),
        "dy": (m * n((T, H)) / np.sqrt(T) / s).astype(np.float32),
        "mom": (n((768, 1024))).astype(np.float32),
    }


def reference(x4_words, x4_scales, x8, dy, mom):
    x4_ = unpack_weight(x4_words, x4_scales, "e2m1")
    x8_ = mxq(f64(x8), 0, "e4m3")
    dy_ = mxq(f64(dy), 0, "e5m2")
    y = x4_.T @ dy_[:O] + x8_.T @ dy_[O:]
    return 0.9 * f64(mom) + y

@@ -1,0 +1,134 @@
+from contextlib import ExitStack
+
+import concourse.mybir as mybir
+
+T4, T8, D, H = 1024, 512, 768, 1024
+FLOPS = 2 * (T4 + T8) * D * H
+
+F32 = mybir.dt.float32
+BF16 = mybir.dt.bfloat16
+I32 = mybir.dt.int32
+U32 = mybir.dt.uint32
+U8 = mybir.dt.uint8
+E4M3 = mybir.dt.float8_e4m3fn_x4
+E5M2 = mybir.dt.float8_e5m2_x4
+E2M1 = mybir.dt.float4_e2m1fn_x4
+MULT = mybir.AluOpType.mult
+ADD = mybir.AluOpType.add
+
+P = 128
+PACK = 4
+NT = 512
+DT = D // P
+HT = H // NT
+BANKS = 8
+V_COLS = 640
+
+
+def interleave(copy, grouped, raw, w0, w1):
+    copy(
+        out=grouped[:, w0:w1, :].rearrange("p (c i) j -> p c j i", i=4),
+        in_=raw[:, :, w0:w1].rearrange("p j (c i) -> p c j i", i=4),
+    )
+
+
+def tile_mix_dwsav_ema_kernel(tc, x4_words, x4_scales, x8, dy, mom, out):
+    nc = tc.nc
+    with ExitStack() as ctx:
+        keep = ctx.enter_context(tc.tile_pool(name="keep", bufs=1))
+        psum = ctx.enter_context(tc.psum_pool(name="psum", bufs=1))
+        ctx.enter_context(tc.manual_schedule())
+
+        x4_codes = keep.tile([P, 2, 2 * D], U8, align_bytes=256)
+        x4_plane = keep.tile([P, 2, D], U8, align_bytes=256)
+        x8_raw = keep.tile([P, PACK, D], F32, align_bytes=256)
+        x8_grouped = keep.tile([P, D, PACK], BF16, align_bytes=256)
+        x8_codes = keep.tile([P, D], U32, align_bytes=256)
+        x8_plane = keep.tile([P, D], U8, align_bytes=256)
+        mom_sb = keep.tile([P, DT, H], F32, align_bytes=256)
+        res = keep.tile([P, DT, H], F32, align_bytes=256)
+        dy_raw, dy_grouped, dy_codes, dy_plane = [], [], [], []
+        for a in range(3):
+            dy_raw.append(keep.tile([P, PACK, H], F32, align_bytes=256, name="dy_raw%d" % a))
+            dy_grouped.append(keep.tile([P, H, PACK], BF16, align_bytes=256, name="dy_grouped%d" % a))
+            dy_codes.append(keep.tile([P, H], U32, align_bytes=256, name="dy_codes%d" % a))
+            dy_plane.append(keep.tile([P, H], U8, align_bytes=256, name="dy_plane%d" % a))
+
+        nc.vector.memset(x4_plane[:].rearrange("p a n -> p (a n)").bitcast(I32), 0)
+
+        nc.sync.dma_start(out=x4_codes[:].bitcast(I32), in_=x4_words.rearrange("a p n -> p a n").bitcast(I32))
+        nc.sync.dma_start(out=x8_raw[:], in_=x8.rearrange("(p j) d -> p j d", j=PACK))
+        for q in range(4):
+            nc.sync.dma_start(
+                out=x4_plane[32 * q : 32 * q + 4, :, :].bitcast(I32),
+                in_=x4_scales[:, 4 * q : 4 * q + 4, :].rearrange("a r n -> r a n").bitcast(I32),
+            )
+        for a in range(3):
+            nc.sync.dma_start(out=dy_raw[a][:], in_=dy[512 * a : 512 * (a + 1), :].rearrange("(p j) h -> p j h", j=PACK))
+        for m in range(0, DT, 2):
+            nc.sync.dma_start(
+                out=mom_sb[:, m : m + 2, :],
+                in_=mom[P * m : P * (m + 2), :].rearrange("(m p) h -> p m h", p=P),
+            )
+
+        def quantize(codes, plane, grouped, fmt, w0, w1):
+            nc.vector.quantize_mx(
+                out=codes[:, w0:w1].bitcast(fmt),
+                scales=plane[:, w0:w1],
+                in_=grouped[:, w0:w1, :].rearrange("p w j -> p (w j)"),
+            )
+
+        for w0, w1 in ((0, 512), (512, 768)):
+            interleave(nc.scalar.copy, x8_grouped, x8_raw, w0, w1)
+        for w0, w1 in ((0, 512), (512, 768)):
+            quantize(x8_codes, x8_plane, x8_grouped, E4M3, w0, w1)
+
+        def stationary(a, m):
+            cols = slice(P * m, P * (m + 1))
+            if a < 2:
+                return x4_codes[:, a, 2 * P * m : 2 * P * (m + 1)].bitcast(E2M1), x4_plane[:, a, cols]
+            return x8_codes[:, cols].bitcast(E4M3), x8_plane[:, cols]
+
+        acc = {}
+
+        def multiply(a, m, h):
+            if a == 0:
+                bank = (HT * m + h) % BANKS
+                acc[(m, h)] = psum.tile([P, NT], F32, name="acc%d" % bank)
+            codes, plane = stationary(a, m)
+            cols = slice(NT * h, NT * (h + 1))
+            nc.tensor.matmul_mx(
+                out=acc[(m, h)][:],
+                lhsT=codes,
+                lhsT_scale=plane,
+                rhs=dy_codes[a][:, cols].bitcast(E5M2),
+                rhs_scale=dy_plane[a][:, cols],
+                start=(a == 0),
+                stop=(a == 2),
+            )
+
+        def finish(m):
+            for h in range(HT):
+                cols = slice(NT * h, NT * (h + 1))
+                nc.vector.scalar_tensor_tensor(
+                    out=res[:, m, cols], in0=mom_sb[:, m, cols], scalar=0.9, in1=acc[(m, h)][:], op0=MULT, op1=ADD
+                )
+            nc.sync.dma_start(out=out[P * m : P * (m + 1), :], in_=res[:, m, :])
+
+        early = BANKS // HT
+        for a in range(3):
+            interleave(nc.scalar.copy, dy_grouped[a], dy_raw[a], V_COLS, H)
+            interleave(nc.vector.tensor_copy, dy_grouped[a], dy_raw[a], 0, NT)
+            interleave(nc.vector.tensor_copy, dy_grouped[a], dy_raw[a], NT, V_COLS)
+            for h in range(HT):
+                quantize(dy_codes[a], dy_plane[a], dy_grouped[a], E5M2, NT * h, NT * (h + 1))
+            for m in range(early):
+                for h in range(HT):
+                    multiply(a, m, h)
+        for m in range(early):
+            finish(m)
+        for m in range(early, DT):
+            for h in range(HT):
+                for a in range(3):
+                    multiply(a, m, h)
+            finish(m)

@@ -58,10 +58,10 @@ def tile_mix_dwsav_ema_kernel(tc, x4_words, x4_scales, x8, dy, mom, out):
 
         nc.sync.dma_start(out=x4_codes[:].bitcast(I32), in_=x4_words.rearrange("a p n -> p a n").bitcast(I32))
         nc.sync.dma_start(out=x8_raw[:], in_=x8.rearrange("(p j) d -> p j d", j=PACK))
-        for q in range(4):
+        for r in range(4):
             nc.sync.dma_start(
-                out=x4_plane[32 * q : 32 * q + 4, :, :].bitcast(I32),
-                in_=x4_scales[:, 4 * q : 4 * q + 4, :].rearrange("a r n -> r a n").bitcast(I32),
+                out=x4_plane[r:P:32, :, :].bitcast(I32),
+                in_=x4_scales[:, r:16:4, :].rearrange("a q n -> q a n").bitcast(I32),
             )
         for a in range(3):
             nc.sync.dma_start(out=dy_raw[a][:], in_=dy[512 * a : 512 * (a + 1), :].rearrange("(p j) h -> p j h", j=PACK))

@@ -56,20 +56,21 @@ def tile_mix_dwsav_ema_kernel(tc, x4_words, x4_scales, x8, dy, mom, out):
 
         nc.vector.memset(x4_plane[:].rearrange("p a n -> p (a n)").bitcast(I32), 0)
 
+        def load_dy(a):
+            nc.sync.dma_start(out=dy_raw[a][:], in_=dy[512 * a : 512 * (a + 1), :].rearrange("(p j) h -> p j h", j=PACK))
+
         nc.sync.dma_start(out=x4_codes[:].bitcast(I32), in_=x4_words.rearrange("a p n -> p a n").bitcast(I32))
-        nc.sync.dma_start(out=x8_raw[:], in_=x8.rearrange("(p j) d -> p j d", j=PACK))
+        load_dy(2)
         for r in range(4):
             nc.sync.dma_start(
                 out=x4_plane[r:P:32, :, :].bitcast(I32),
                 in_=x4_scales[:, r:16:4, :].rearrange("a q n -> q a n").bitcast(I32),
             )
-        for a in range(3):
-            nc.sync.dma_start(out=dy_raw[a][:], in_=dy[512 * a : 512 * (a + 1), :].rearrange("(p j) h -> p j h", j=PACK))
-        for m in range(0, DT, 2):
-            nc.sync.dma_start(
-                out=mom_sb[:, m : m + 2, :],
-                in_=mom[P * m : P * (m + 2), :].rearrange("(m p) h -> p m h", p=P),
-            )
+        load_dy(0)
+        load_dy(1)
+        nc.sync.dma_start(out=x8_raw[:], in_=x8.rearrange("(p j) d -> p j d", j=PACK))
+        for m in range(DT):
+            nc.sync.dma_start(out=mom_sb[:, m, :], in_=mom[P * m : P * (m + 1), :])
 
         def quantize(codes, plane, grouped, fmt, w0, w1):
             nc.vector.quantize_mx(
@@ -77,11 +78,6 @@ def tile_mix_dwsav_ema_kernel(tc, x4_words, x4_scales, x8, dy, mom, out):
                 scales=plane[:, w0:w1],
                 in_=grouped[:, w0:w1, :].rearrange("p w j -> p (w j)"),
             )
-
-        for w0, w1 in ((0, 512), (512, 768)):
-            interleave(nc.scalar.copy, x8_grouped, x8_raw, w0, w1)
-        for w0, w1 in ((0, 512), (512, 768)):
-            quantize(x8_codes, x8_plane, x8_grouped, E4M3, w0, w1)
 
         def stationary(a, m):
             cols = slice(P * m, P * (m + 1))
@@ -107,28 +103,51 @@ def tile_mix_dwsav_ema_kernel(tc, x4_words, x4_scales, x8, dy, mom, out):
                 stop=(a == 2),
             )
 
-        def finish(m):
-            for h in range(HT):
-                cols = slice(NT * h, NT * (h + 1))
-                nc.vector.scalar_tensor_tensor(
-                    out=res[:, m, cols], in0=mom_sb[:, m, cols], scalar=0.9, in1=acc[(m, h)][:], op0=MULT, op1=ADD
-                )
-            nc.sync.dma_start(out=out[P * m : P * (m + 1), :], in_=res[:, m, :])
+        def finish(m, h):
+            cols = slice(NT * h, NT * (h + 1))
+            nc.vector.scalar_tensor_tensor(
+                out=res[:, m, cols], in0=mom_sb[:, m, cols], scalar=0.9, in1=acc[(m, h)][:], op0=MULT, op1=ADD
+            )
+            if h == HT - 1:
+                nc.sync.dma_start(out=out[P * m : P * (m + 1), :], in_=res[:, m, :])
+
+        def quantize_x8(m0, m1):
+            quantize(x8_codes, x8_plane, x8_grouped, E4M3, P * m0, P * m1)
 
         early = BANKS // HT
-        for a in range(3):
+        for a in (2, 0, 1):
             interleave(nc.scalar.copy, dy_grouped[a], dy_raw[a], V_COLS, H)
             interleave(nc.vector.tensor_copy, dy_grouped[a], dy_raw[a], 0, NT)
             interleave(nc.vector.tensor_copy, dy_grouped[a], dy_raw[a], NT, V_COLS)
             for h in range(HT):
                 quantize(dy_codes[a], dy_plane[a], dy_grouped[a], E5M2, NT * h, NT * (h + 1))
-            for m in range(early):
+            if a < 2:
                 for h in range(HT):
-                    multiply(a, m, h)
-        for m in range(early):
-            finish(m)
+                    for m in range(early):
+                        multiply(a, m, h)
+
+        interleave(nc.vector.tensor_copy, x8_grouped, x8_raw, 0, P)
+        for m in range(1, DT):
+            interleave(nc.scalar.copy, x8_grouped, x8_raw, P * m, P * (m + 1))
+        quantize_x8(0, 1)
+        quantize_x8(1, 2)
+        for m in (0, 1):
+            for h in range(HT):
+                multiply(2, m, h)
+        quantize_x8(2, 3)
+        finish(0, 0)
+        quantize_x8(3, 4)
+        for m in (2, 3):
+            for h in range(HT):
+                multiply(2, m, h)
+        finish(0, 1)
+        quantize_x8(4, 6)
+        for h in range(HT):
+            finish(1, h)
         for m in range(early, DT):
             for h in range(HT):
                 for a in range(3):
                     multiply(a, m, h)
-            finish(m)
+        for m in range(2, DT):
+            for h in range(HT):
+                finish(m, h)

@@ -40,6 +40,8 @@ def tile_mix_dwsav_ema_kernel(tc, x4_words, x4_scales, x8, dy, mom, out):
         ctx.enter_context(tc.manual_schedule())
 
         x4_codes = keep.tile([P, 2, 2 * D], U8, align_bytes=256)
+        x4_codes_raw = keep.tile([P, 2, 2 * D], U8, align_bytes=256)
+        x4_plane_raw = keep.tile([P, 2, D], U8, align_bytes=256)
         x4_plane = keep.tile([P, 2, D], U8, align_bytes=256)
         x8_raw = keep.tile([P, PACK, D], F32, align_bytes=256)
         x8_grouped = keep.tile([P, D, PACK], BF16, align_bytes=256)
@@ -54,23 +56,31 @@ def tile_mix_dwsav_ema_kernel(tc, x4_words, x4_scales, x8, dy, mom, out):
             dy_codes.append(keep.tile([P, H], U32, align_bytes=256, name="dy_codes%d" % a))
             dy_plane.append(keep.tile([P, H], U8, align_bytes=256, name="dy_plane%d" % a))
 
-        nc.vector.memset(x4_plane[:].rearrange("p a n -> p (a n)").bitcast(I32), 0)
+        nc.vector.memset(x4_plane_raw[:].rearrange("p a n -> p (a n)").bitcast(I32), 0)
 
         def load_dy(a):
             nc.sync.dma_start(out=dy_raw[a][:], in_=dy[512 * a : 512 * (a + 1), :].rearrange("(p j) h -> p j h", j=PACK))
 
-        nc.sync.dma_start(out=x4_codes[:].bitcast(I32), in_=x4_words.rearrange("a p n -> p a n").bitcast(I32))
+        nc.sync.dma_start(out=x4_codes_raw[:].bitcast(I32), in_=x4_words.rearrange("a p n -> p a n").bitcast(I32))
         load_dy(2)
         for r in range(4):
             nc.sync.dma_start(
-                out=x4_plane[r:P:32, :, :].bitcast(I32),
+                out=x4_plane_raw[r:P:32, :, :].bitcast(I32),
                 in_=x4_scales[:, r:16:4, :].rearrange("a q n -> q a n").bitcast(I32),
             )
         load_dy(0)
         load_dy(1)
         nc.sync.dma_start(out=x8_raw[:], in_=x8.rearrange("(p j) d -> p j d", j=PACK))
-        for m in range(DT):
-            nc.sync.dma_start(out=mom_sb[:, m, :], in_=mom[P * m : P * (m + 1), :])
+        for m in range(0, DT, 2):
+            nc.sync.dma_start(
+                out=mom_sb[:, m : m + 2, :],
+                in_=mom[P * m : P * (m + 2), :].rearrange("(p e) h -> p e h", e=2),
+            )
+
+        nc.vector.tensor_copy(
+            out=x4_codes[:].rearrange("p a (s e q b) -> p (a s) e q b", e=2, q=P, b=2),
+            in_=x4_codes_raw[:].rearrange("p a (s q e b) -> p (a s) e q b", e=2, q=P, b=2),
+        )
 
         def quantize(codes, plane, grouped, fmt, w0, w1):
             nc.vector.quantize_mx(
@@ -103,13 +113,15 @@ def tile_mix_dwsav_ema_kernel(tc, x4_words, x4_scales, x8, dy, mom, out):
                 stop=(a == 2),
             )
 
+        out_rows = out.rearrange("(s p e) h -> s p e h", p=P, e=2)
+
         def finish(m, h):
             cols = slice(NT * h, NT * (h + 1))
             nc.vector.scalar_tensor_tensor(
                 out=res[:, m, cols], in0=mom_sb[:, m, cols], scalar=0.9, in1=acc[(m, h)][:], op0=MULT, op1=ADD
             )
             if h == HT - 1:
-                nc.sync.dma_start(out=out[P * m : P * (m + 1), :], in_=res[:, m, :])
+                nc.sync.dma_start(out=out_rows[m // 2, :, m % 2, :], in_=res[:, m, :])
 
         def quantize_x8(m0, m1):
             quantize(x8_codes, x8_plane, x8_grouped, E4M3, P * m0, P * m1)
@@ -121,14 +133,26 @@ def tile_mix_dwsav_ema_kernel(tc, x4_words, x4_scales, x8, dy, mom, out):
             interleave(nc.vector.tensor_copy, dy_grouped[a], dy_raw[a], NT, V_COLS)
             for h in range(HT):
                 quantize(dy_codes[a], dy_plane[a], dy_grouped[a], E5M2, NT * h, NT * (h + 1))
+            if a == 2:
+                nc.vector.tensor_copy(
+                    out=x4_plane[:].rearrange("p a (s e q) -> p (a s) e q", e=2, q=P),
+                    in_=x4_plane_raw[:].rearrange("p a (s q e) -> p (a s) e q", e=2, q=P),
+                )
             if a < 2:
                 for h in range(HT):
                     for m in range(early):
                         multiply(a, m, h)
 
-        interleave(nc.vector.tensor_copy, x8_grouped, x8_raw, 0, P)
+        def interleave_x8(copy, m):
+            first = 2 * P * (m // 2) + m % 2
+            copy(
+                out=x8_grouped[:, P * m : P * (m + 1), :].rearrange("p (c i) j -> p c j i", i=2),
+                in_=x8_raw[:, :, first : 2 * P * (m // 2 + 1) : 2].rearrange("p j (c i) -> p c j i", i=2),
+            )
+
+        interleave_x8(nc.vector.tensor_copy, 0)
         for m in range(1, DT):
-            interleave(nc.scalar.copy, x8_grouped, x8_raw, P * m, P * (m + 1))
+            interleave_x8(nc.scalar.copy, m)
         quantize_x8(0, 1)
         quantize_x8(1, 2)
         for m in (0, 1):

@@ -15,6 +15,7 @@ E5M2 = mybir.dt.float8_e5m2_x4
 E2M1 = mybir.dt.float4_e2m1fn_x4
 MULT = mybir.AluOpType.mult
 ADD = mybir.AluOpType.add
+COPY = mybir.ActivationFunctionType.Copy
 
 P = 128
 PACK = 4
@@ -49,6 +50,8 @@ def tile_mix_dwsav_ema_kernel(tc, x4_words, x4_scales, x8, dy, mom, out):
         x8_plane = keep.tile([P, D], U8, align_bytes=256)
         mom_sb = keep.tile([P, DT, H], F32, align_bytes=256)
         res = keep.tile([P, DT, H], F32, align_bytes=256)
+        sums = keep.tile([P, DT // 2, NT], F32, align_bytes=256)
+        decayed = keep.tile([P, DT // 2, NT], F32, align_bytes=256)
         dy_raw, dy_grouped, dy_codes, dy_plane = [], [], [], []
         for a in range(3):
             dy_raw.append(keep.tile([P, PACK, H], F32, align_bytes=256, name="dy_raw%d" % a))
@@ -120,8 +123,18 @@ def tile_mix_dwsav_ema_kernel(tc, x4_words, x4_scales, x8, dy, mom, out):
             nc.vector.scalar_tensor_tensor(
                 out=res[:, m, cols], in0=mom_sb[:, m, cols], scalar=0.9, in1=acc[(m, h)][:], op0=MULT, op1=ADD
             )
-            if h == HT - 1:
-                nc.sync.dma_start(out=out_rows[m // 2, :, m % 2, :], in_=res[:, m, :])
+
+        def finish_on_scalar_and_gpsimd(m, h):
+            cols = slice(NT * h, NT * (h + 1))
+            nc.scalar.copy(out=sums[:, m // 2, :], in_=acc[(m, h)][:])
+            nc.scalar.activation(out=decayed[:, m // 2, :], in_=mom_sb[:, m, cols], func=COPY, scale=0.9)
+            nc.gpsimd.tensor_tensor(out=res[:, m, cols], in0=decayed[:, m // 2, :], in1=sums[:, m // 2, :], op=ADD)
+
+        def store_tile(m):
+            nc.sync.dma_start(out=out_rows[m // 2, :, m % 2, :], in_=res[:, m, :])
+
+        def store_pair(s):
+            nc.sync.dma_start(out=out_rows[s], in_=res[:, 2 * s : 2 * s + 2, :])
 
         def quantize_x8(m0, m1):
             quantize(x8_codes, x8_plane, x8_grouped, E4M3, P * m0, P * m1)
@@ -165,13 +178,22 @@ def tile_mix_dwsav_ema_kernel(tc, x4_words, x4_scales, x8, dy, mom, out):
             for h in range(HT):
                 multiply(2, m, h)
         finish(0, 1)
+        store_tile(0)
         quantize_x8(4, 6)
         for h in range(HT):
             finish(1, h)
+        store_tile(1)
+        finish_on_scalar_and_gpsimd(2, 0)
         for m in range(early, DT):
             for h in range(HT):
                 for a in range(3):
                     multiply(a, m, h)
-        for m in range(2, DT):
-            for h in range(HT):
-                finish(m, h)
+        finish(2, 1)
+        finish(3, 0)
+        finish(3, 1)
+        store_pair(1)
+        finish_on_scalar_and_gpsimd(4, 0)
+        finish(4, 1)
+        finish(5, 0)
+        finish(5, 1)
+        store_pair(2)

@@ -163,26 +163,23 @@ def tile_mix_dwsav_ema_kernel(tc, x4_words, x4_scales, x8, dy, mom, out):
                 in_=x8_raw[:, :, first : 2 * P * (m // 2 + 1) : 2].rearrange("p j (c i) -> p c j i", i=2),
             )
 
-        interleave_x8(nc.vector.tensor_copy, 0)
-        for m in range(1, DT):
+        for m in (1, 2, 3):
             interleave_x8(nc.scalar.copy, m)
+        interleave_x8(nc.vector.tensor_copy, 0)
+        interleave_x8(nc.vector.tensor_copy, 4)
         quantize_x8(0, 1)
         quantize_x8(1, 2)
+        interleave_x8(nc.vector.tensor_copy, 5)
+        quantize_x8(2, 3)
+        quantize_x8(4, 6)
+        quantize_x8(3, 4)
+        for m in range(early):
+            for h in range(HT):
+                multiply(2, m, h)
         for m in (0, 1):
             for h in range(HT):
-                multiply(2, m, h)
-        quantize_x8(2, 3)
-        finish(0, 0)
-        quantize_x8(3, 4)
-        for m in (2, 3):
-            for h in range(HT):
-                multiply(2, m, h)
-        finish(0, 1)
-        store_tile(0)
-        quantize_x8(4, 6)
-        for h in range(HT):
-            finish(1, h)
-        store_tile(1)
+                finish(m, h)
+            store_tile(m)
         finish_on_scalar_and_gpsimd(2, 0)
         for m in range(early, DT):
             for h in range(HT):

@@ -130,9 +130,6 @@ def tile_mix_dwsav_ema_kernel(tc, x4_words, x4_scales, x8, dy, mom, out):
             nc.scalar.activation(out=decayed[:, m // 2, :], in_=mom_sb[:, m, cols], func=COPY, scale=0.9)
             nc.gpsimd.tensor_tensor(out=res[:, m, cols], in0=decayed[:, m // 2, :], in1=sums[:, m // 2, :], op=ADD)
 
-        def store_tile(m):
-            nc.sync.dma_start(out=out_rows[m // 2, :, m % 2, :], in_=res[:, m, :])
-
         def store_pair(s):
             nc.sync.dma_start(out=out_rows[s], in_=res[:, 2 * s : 2 * s + 2, :])
 
@@ -163,23 +160,25 @@ def tile_mix_dwsav_ema_kernel(tc, x4_words, x4_scales, x8, dy, mom, out):
                 in_=x8_raw[:, :, first : 2 * P * (m // 2 + 1) : 2].rearrange("p j (c i) -> p c j i", i=2),
             )
 
-        for m in (1, 2, 3):
-            interleave_x8(nc.scalar.copy, m)
+        interleave_x8(nc.scalar.copy, 1)
+        interleave_x8(nc.scalar.copy, 2)
         interleave_x8(nc.vector.tensor_copy, 0)
-        interleave_x8(nc.vector.tensor_copy, 4)
+        interleave_x8(nc.vector.tensor_copy, 3)
         quantize_x8(0, 1)
         quantize_x8(1, 2)
-        interleave_x8(nc.vector.tensor_copy, 5)
-        quantize_x8(2, 3)
-        quantize_x8(4, 6)
-        quantize_x8(3, 4)
+        interleave_x8(nc.vector.tensor_copy, 4)
+        quantize_x8(2, 4)
+        quantize_x8(4, 5)
         for m in range(early):
             for h in range(HT):
                 multiply(2, m, h)
-        for m in (0, 1):
-            for h in range(HT):
-                finish(m, h)
-            store_tile(m)
+        finish_on_scalar_and_gpsimd(0, 0)
+        interleave_x8(nc.scalar.copy, 5)
+        finish(0, 1)
+        finish(1, 0)
+        finish(1, 1)
+        store_pair(0)
+        quantize_x8(5, 6)
         finish_on_scalar_and_gpsimd(2, 0)
         for m in range(early, DT):
             for h in range(HT):

@@ -151,7 +151,8 @@ def tile_mix_dwsav_ema_kernel(tc, x4_words, x4_scales, x8, dy, mom, out):
             if a < 2:
                 for h in range(HT):
                     for m in range(early):
-                        multiply(a, m, h)
+                        if (a, h) != (1, 1) or m < 2:
+                            multiply(a, m, h)
 
         def interleave_x8(copy, m):
             first = 2 * P * (m // 2) + m % 2
@@ -171,6 +172,8 @@ def tile_mix_dwsav_ema_kernel(tc, x4_words, x4_scales, x8, dy, mom, out):
         quantize_x8(4, 5)
         for m in range(early):
             for h in range(HT):
+                if m >= 2 and h == 1:
+                    multiply(1, m, h)
                 multiply(2, m, h)
         finish_on_scalar_and_gpsimd(0, 0)
         interleave_x8(nc.scalar.copy, 5)

@@ -23,7 +23,6 @@ NT = 512
 DT = D // P
 HT = H // NT
 BANKS = 8
-V_COLS = 640
 
 
 def interleave(copy, grouped, raw, w0, w1):
@@ -42,6 +41,7 @@ def tile_mix_dwsav_ema_kernel(tc, x4_words, x4_scales, x8, dy, mom, out):
 
         x4_codes = keep.tile([P, 2, 2 * D], U8, align_bytes=256)
         x4_codes_raw = keep.tile([P, 2, 2 * D], U8, align_bytes=256)
+        x4_rows = keep.tile([P, 2, D], U8, align_bytes=256)
         x4_plane_raw = keep.tile([P, 2, D], U8, align_bytes=256)
         x4_plane = keep.tile([P, 2, D], U8, align_bytes=256)
         x8_raw = keep.tile([P, PACK, D], F32, align_bytes=256)
@@ -52,27 +52,25 @@ def tile_mix_dwsav_ema_kernel(tc, x4_words, x4_scales, x8, dy, mom, out):
         res = keep.tile([P, DT, H], F32, align_bytes=256)
         sums = keep.tile([P, DT // 2, NT], F32, align_bytes=256)
         decayed = keep.tile([P, DT // 2, NT], F32, align_bytes=256)
-        dy_raw, dy_grouped, dy_codes, dy_plane = [], [], [], []
+        dy_raw4 = keep.tile([P, 2, PACK, H], F32, align_bytes=256)
+        dy_raw8 = keep.tile([P, PACK, H], F32, align_bytes=256)
+        dy_raw = [dy_raw4[:, 0], dy_raw4[:, 1], dy_raw8[:]]
+        dy_grouped, dy_codes, dy_plane = [], [], []
         for a in range(3):
-            dy_raw.append(keep.tile([P, PACK, H], F32, align_bytes=256, name="dy_raw%d" % a))
             dy_grouped.append(keep.tile([P, H, PACK], BF16, align_bytes=256, name="dy_grouped%d" % a))
             dy_codes.append(keep.tile([P, H], U32, align_bytes=256, name="dy_codes%d" % a))
             dy_plane.append(keep.tile([P, H], U8, align_bytes=256, name="dy_plane%d" % a))
 
         nc.vector.memset(x4_plane_raw[:].rearrange("p a n -> p (a n)").bitcast(I32), 0)
 
-        def load_dy(a):
-            nc.sync.dma_start(out=dy_raw[a][:], in_=dy[512 * a : 512 * (a + 1), :].rearrange("(p j) h -> p j h", j=PACK))
-
         nc.sync.dma_start(out=x4_codes_raw[:].bitcast(I32), in_=x4_words.rearrange("a p n -> p a n").bitcast(I32))
-        load_dy(2)
         for r in range(4):
             nc.sync.dma_start(
-                out=x4_plane_raw[r:P:32, :, :].bitcast(I32),
+                out=x4_rows[r:P:32, :, :].bitcast(I32),
                 in_=x4_scales[:, r:16:4, :].rearrange("a q n -> q a n").bitcast(I32),
             )
-        load_dy(0)
-        load_dy(1)
+        nc.sync.dma_start(out=dy_raw4[:], in_=dy[:T4, :].rearrange("(a p j) h -> p a j h", a=2, j=PACK))
+        nc.sync.dma_start(out=dy_raw8[:], in_=dy[T4:, :].rearrange("(p j) h -> p j h", j=PACK))
         nc.sync.dma_start(out=x8_raw[:], in_=x8.rearrange("(p j) d -> p j d", j=PACK))
         for m in range(0, DT, 2):
             nc.sync.dma_start(
@@ -83,6 +81,12 @@ def tile_mix_dwsav_ema_kernel(tc, x4_words, x4_scales, x8, dy, mom, out):
         nc.vector.tensor_copy(
             out=x4_codes[:].rearrange("p a (s e q b) -> p (a s) e q b", e=2, q=P, b=2),
             in_=x4_codes_raw[:].rearrange("p a (s q e b) -> p (a s) e q b", e=2, q=P, b=2),
+        )
+        for q in range(0, P, 32):
+            nc.vector.tensor_copy(out=x4_plane_raw[q : q + 4].bitcast(I32), in_=x4_rows[q : q + 4].bitcast(I32))
+        nc.vector.tensor_copy(
+            out=x4_plane[:].rearrange("p a (s e q) -> p (a s) e q", e=2, q=P),
+            in_=x4_plane_raw[:].rearrange("p a (s q e) -> p (a s) e q", e=2, q=P),
         )
 
         def quantize(codes, plane, grouped, fmt, w0, w1):
@@ -137,22 +141,24 @@ def tile_mix_dwsav_ema_kernel(tc, x4_words, x4_scales, x8, dy, mom, out):
             quantize(x8_codes, x8_plane, x8_grouped, E4M3, P * m0, P * m1)
 
         early = BANKS // HT
-        for a in (2, 0, 1):
-            interleave(nc.scalar.copy, dy_grouped[a], dy_raw[a], V_COLS, H)
-            interleave(nc.vector.tensor_copy, dy_grouped[a], dy_raw[a], 0, NT)
-            interleave(nc.vector.tensor_copy, dy_grouped[a], dy_raw[a], NT, V_COLS)
-            for h in range(HT):
-                quantize(dy_codes[a], dy_plane[a], dy_grouped[a], E5M2, NT * h, NT * (h + 1))
-            if a == 2:
-                nc.vector.tensor_copy(
-                    out=x4_plane[:].rearrange("p a (s e q) -> p (a s) e q", e=2, q=P),
-                    in_=x4_plane_raw[:].rearrange("p a (s q e) -> p (a s) e q", e=2, q=P),
-                )
+        for a in range(3):
+            interleave(nc.scalar.copy, dy_grouped[a], dy_raw[a], NT, H)
+
+        def quantize_dy(a, h):
+            quantize(dy_codes[a], dy_plane[a], dy_grouped[a], E5M2, NT * h, NT * (h + 1))
             if a < 2:
-                for h in range(HT):
-                    for m in range(early):
-                        if (a, h) != (1, 1) or m < 2:
-                            multiply(a, m, h)
+                for m in range(early):
+                    multiply(a, m, h)
+
+        interleave(nc.vector.tensor_copy, dy_grouped[0], dy_raw[0], 0, NT)
+        interleave(nc.vector.tensor_copy, dy_grouped[1], dy_raw[1], 0, NT)
+        quantize_dy(0, 0)
+        quantize_dy(0, 1)
+        quantize_dy(1, 0)
+        interleave(nc.vector.tensor_copy, dy_grouped[2], dy_raw[2], 0, NT)
+        quantize_dy(1, 1)
+        quantize_dy(2, 0)
+        quantize_dy(2, 1)
 
         def interleave_x8(copy, m):
             first = 2 * P * (m // 2) + m % 2
@@ -172,8 +178,6 @@ def tile_mix_dwsav_ema_kernel(tc, x4_words, x4_scales, x8, dy, mom, out):
         quantize_x8(4, 5)
         for m in range(early):
             for h in range(HT):
-                if m >= 2 and h == 1:
-                    multiply(1, m, h)
                 multiply(2, m, h)
         finish_on_scalar_and_gpsimd(0, 0)
         interleave_x8(nc.scalar.copy, 5)

@@ -65,7 +65,7 @@ def tile_mix_dwsav_ema_kernel(tc, x4_words, x4_scales, x8, dy, mom, out):
 
         nc.sync.dma_start(out=x4_codes_raw[:].bitcast(I32), in_=x4_words.rearrange("a p n -> p a n").bitcast(I32))
         for r in range(4):
-            nc.sync.dma_start(
+            (nc.scalar if r < 2 else nc.sync).dma_start(
                 out=x4_rows[r:P:32, :, :].bitcast(I32),
                 in_=x4_scales[:, r:16:4, :].rearrange("a q n -> q a n").bitcast(I32),
             )

@@ -61,7 +61,7 @@ def tile_mix_dwsav_ema_kernel(tc, x4_words, x4_scales, x8, dy, mom, out):
             dy_codes.append(keep.tile([P, H], U32, align_bytes=256, name="dy_codes%d" % a))
             dy_plane.append(keep.tile([P, H], U8, align_bytes=256, name="dy_plane%d" % a))
 
-        nc.vector.memset(x4_plane_raw[:].rearrange("p a n -> p (a n)").bitcast(I32), 0)
+        nc.gpsimd.memset(x4_plane_raw[:].rearrange("p a n -> p (a n)").bitcast(I32), 0)
 
         nc.sync.dma_start(out=x4_codes_raw[:].bitcast(I32), in_=x4_words.rearrange("a p n -> p a n").bitcast(I32))
         for r in range(4):
@@ -83,8 +83,8 @@ def tile_mix_dwsav_ema_kernel(tc, x4_words, x4_scales, x8, dy, mom, out):
             in_=x4_codes_raw[:].rearrange("p a (s q e b) -> p (a s) e q b", e=2, q=P, b=2),
         )
         for q in range(0, P, 32):
-            nc.vector.tensor_copy(out=x4_plane_raw[q : q + 4].bitcast(I32), in_=x4_rows[q : q + 4].bitcast(I32))
-        nc.vector.tensor_copy(
+            nc.gpsimd.tensor_copy(out=x4_plane_raw[q : q + 4].bitcast(I32), in_=x4_rows[q : q + 4].bitcast(I32))
+        nc.gpsimd.tensor_copy(
             out=x4_plane[:].rearrange("p a (s e q) -> p (a s) e q", e=2, q=P),
             in_=x4_plane_raw[:].rearrange("p a (s q e) -> p (a s) e q", e=2, q=P),
         )

@@ -64,11 +64,13 @@ def tile_mix_dwsav_ema_kernel(tc, x4_words, x4_scales, x8, dy, mom, out):
         nc.gpsimd.memset(x4_plane_raw[:].rearrange("p a n -> p (a n)").bitcast(I32), 0)
 
         nc.sync.dma_start(out=x4_codes_raw[:].bitcast(I32), in_=x4_words.rearrange("a p n -> p a n").bitcast(I32))
-        for r in range(4):
+        for r in range(3):
             (nc.scalar if r < 2 else nc.sync).dma_start(
                 out=x4_rows[r:P:32, :, :].bitcast(I32),
                 in_=x4_scales[:, r:16:4, :].rearrange("a q n -> q a n").bitcast(I32),
             )
+        for a in range(2):
+            nc.sync.dma_start(out=x4_rows[3:P:32, a, :].bitcast(I32), in_=x4_scales[a, 3:16:4, :].bitcast(I32))
         nc.sync.dma_start(out=dy_raw4[:], in_=dy[:T4, :].rearrange("(a p j) h -> p a j h", a=2, j=PACK))
         nc.sync.dma_start(out=dy_raw8[:], in_=dy[T4:, :].rearrange("(p j) h -> p j h", j=PACK))
         nc.sync.dma_start(out=x8_raw[:], in_=x8.rearrange("(p j) d -> p j d", j=PACK))

@@ -23,6 +23,7 @@ NT = 512
 DT = D // P
 HT = H // NT
 BANKS = 8
+WIDTH = DT * H
 
 
 def interleave(copy, grouped, raw, w0, w1):
@@ -48,10 +49,10 @@ def tile_mix_dwsav_ema_kernel(tc, x4_words, x4_scales, x8, dy, mom, out):
         x8_grouped = keep.tile([P, D, PACK], BF16, align_bytes=256)
         x8_codes = keep.tile([P, D], U32, align_bytes=256)
         x8_plane = keep.tile([P, D], U8, align_bytes=256)
-        mom_sb = keep.tile([P, DT, H], F32, align_bytes=256)
-        res = keep.tile([P, DT, H], F32, align_bytes=256)
-        sums = keep.tile([P, DT // 2, NT], F32, align_bytes=256)
-        decayed = keep.tile([P, DT // 2, NT], F32, align_bytes=256)
+        mom_sb = keep.tile([P, WIDTH], F32, align_bytes=256)
+        res = keep.tile([P, WIDTH], F32, align_bytes=256)
+        sums = keep.tile([P, WIDTH], F32, align_bytes=256)
+        decayed = keep.tile([P, WIDTH], F32, align_bytes=256)
         dy_raw4 = keep.tile([P, 2, PACK, H], F32, align_bytes=256)
         dy_raw8 = keep.tile([P, PACK, H], F32, align_bytes=256)
         dy_raw = [dy_raw4[:, 0], dy_raw4[:, 1], dy_raw8[:]]
@@ -74,21 +75,22 @@ def tile_mix_dwsav_ema_kernel(tc, x4_words, x4_scales, x8, dy, mom, out):
         nc.sync.dma_start(out=dy_raw4[:], in_=dy[:T4, :].rearrange("(a p j) h -> p a j h", a=2, j=PACK))
         nc.sync.dma_start(out=dy_raw8[:], in_=dy[T4:, :].rearrange("(p j) h -> p j h", j=PACK))
         nc.sync.dma_start(out=x8_raw[:], in_=x8.rearrange("(p j) d -> p j d", j=PACK))
-        for m in range(0, DT, 2):
-            nc.sync.dma_start(
-                out=mom_sb[:, m : m + 2, :],
-                in_=mom[P * m : P * (m + 2), :].rearrange("(p e) h -> p e h", e=2),
-            )
+        mom_rows = mom.rearrange("(p m) h -> p (m h)", m=DT)
+        out_rows = out.rearrange("(p m) h -> p (m h)", m=DT)
+        load_cuts = [0, 1792, 3072, 4992, WIDTH]
+        for c0, c1 in zip(load_cuts, load_cuts[1:]):
+            nc.sync.dma_start(out=mom_sb[:, c0:c1], in_=mom_rows[:, c0:c1])
 
-        nc.vector.tensor_copy(
-            out=x4_codes[:].rearrange("p a (s e q b) -> p (a s) e q b", e=2, q=P, b=2),
-            in_=x4_codes_raw[:].rearrange("p a (s q e b) -> p (a s) e q b", e=2, q=P, b=2),
-        )
+        for a in range(2):
+            nc.vector.tensor_copy(
+                out=x4_codes[:, a, :].rearrange("p (m q b) -> p m q b", m=DT, b=2),
+                in_=x4_codes_raw[:, a, :].rearrange("p (q m b) -> p m q b", m=DT, b=2),
+            )
         for q in range(0, P, 32):
             nc.gpsimd.tensor_copy(out=x4_plane_raw[q : q + 4].bitcast(I32), in_=x4_rows[q : q + 4].bitcast(I32))
         nc.gpsimd.tensor_copy(
-            out=x4_plane[:].rearrange("p a (s e q) -> p (a s) e q", e=2, q=P),
-            in_=x4_plane_raw[:].rearrange("p a (s q e) -> p (a s) e q", e=2, q=P),
+            out=x4_plane[:].rearrange("p a (m q) -> p a m q", m=DT),
+            in_=x4_plane_raw[:].rearrange("p a (q m) -> p a m q", m=DT),
         )
 
         def quantize(codes, plane, grouped, fmt, w0, w1):
@@ -105,15 +107,16 @@ def tile_mix_dwsav_ema_kernel(tc, x4_words, x4_scales, x8, dy, mom, out):
             return x8_codes[:, cols].bitcast(E4M3), x8_plane[:, cols]
 
         acc = {}
+        bank_of = [0, 1, 2, 3, 4, 5, 6, 7, 0, 1, 2, 3]
 
-        def multiply(a, m, h):
+        def multiply(a, u):
+            m, h = divmod(u, HT)
             if a == 0:
-                bank = (HT * m + h) % BANKS
-                acc[(m, h)] = psum.tile([P, NT], F32, name="acc%d" % bank)
+                acc[u] = psum.tile([P, NT], F32, name="acc%d" % bank_of[u])
             codes, plane = stationary(a, m)
             cols = slice(NT * h, NT * (h + 1))
             nc.tensor.matmul_mx(
-                out=acc[(m, h)][:],
+                out=acc[u][:],
                 lhsT=codes,
                 lhsT_scale=plane,
                 rhs=dy_codes[a][:, cols].bitcast(E5M2),
@@ -122,83 +125,104 @@ def tile_mix_dwsav_ema_kernel(tc, x4_words, x4_scales, x8, dy, mom, out):
                 stop=(a == 2),
             )
 
-        out_rows = out.rearrange("(s p e) h -> s p e h", p=P, e=2)
+        def in_bank(c0, c1):
+            u = c0 // NT
+            return acc[u][:, c0 - NT * u : c1 - NT * u]
 
-        def finish(m, h):
-            cols = slice(NT * h, NT * (h + 1))
+        def finish(c0, c1):
             nc.vector.scalar_tensor_tensor(
-                out=res[:, m, cols], in0=mom_sb[:, m, cols], scalar=0.9, in1=acc[(m, h)][:], op0=MULT, op1=ADD
+                out=res[:, c0:c1], in0=mom_sb[:, c0:c1], scalar=0.9, in1=in_bank(c0, c1), op0=MULT, op1=ADD
             )
 
-        def finish_on_scalar_and_gpsimd(m, h):
-            cols = slice(NT * h, NT * (h + 1))
-            nc.scalar.copy(out=sums[:, m // 2, :], in_=acc[(m, h)][:])
-            nc.scalar.activation(out=decayed[:, m // 2, :], in_=mom_sb[:, m, cols], func=COPY, scale=0.9)
-            nc.gpsimd.tensor_tensor(out=res[:, m, cols], in0=decayed[:, m // 2, :], in1=sums[:, m // 2, :], op=ADD)
+        def drain(c0, c1):
+            nc.scalar.copy(out=sums[:, c0:c1], in_=in_bank(c0, c1))
 
-        def store_pair(s):
-            nc.sync.dma_start(out=out_rows[s], in_=res[:, 2 * s : 2 * s + 2, :])
+        def decay_and_add(c0, c1):
+            nc.scalar.activation(out=decayed[:, c0:c1], in_=mom_sb[:, c0:c1], func=COPY, scale=0.9)
+            nc.gpsimd.tensor_tensor(out=res[:, c0:c1], in0=decayed[:, c0:c1], in1=sums[:, c0:c1], op=ADD)
+
+        def store(c0, c1):
+            nc.sync.dma_start(out=out_rows[:, c0:c1], in_=res[:, c0:c1])
 
         def quantize_x8(m0, m1):
             quantize(x8_codes, x8_plane, x8_grouped, E4M3, P * m0, P * m1)
 
-        early = BANKS // HT
-        for a in range(3):
-            interleave(nc.scalar.copy, dy_grouped[a], dy_raw[a], NT, H)
-
-        def quantize_dy(a, h):
-            quantize(dy_codes[a], dy_plane[a], dy_grouped[a], E5M2, NT * h, NT * (h + 1))
-            if a < 2:
-                for m in range(early):
-                    multiply(a, m, h)
-
-        interleave(nc.vector.tensor_copy, dy_grouped[0], dy_raw[0], 0, NT)
-        interleave(nc.vector.tensor_copy, dy_grouped[1], dy_raw[1], 0, NT)
-        quantize_dy(0, 0)
-        quantize_dy(0, 1)
-        quantize_dy(1, 0)
-        interleave(nc.vector.tensor_copy, dy_grouped[2], dy_raw[2], 0, NT)
-        quantize_dy(1, 1)
-        quantize_dy(2, 0)
-        quantize_dy(2, 1)
-
-        def interleave_x8(copy, m):
-            first = 2 * P * (m // 2) + m % 2
+        def interleave_x8(copy, s, q0, q1):
             copy(
-                out=x8_grouped[:, P * m : P * (m + 1), :].rearrange("p (c i) j -> p c j i", i=2),
-                in_=x8_raw[:, :, first : 2 * P * (m // 2 + 1) : 2].rearrange("p j (c i) -> p c j i", i=2),
+                out=x8_grouped[:].rearrange("p (m q) j -> p q j m", m=DT)[:, q0:q1, :, 2 * s : 2 * s + 2],
+                in_=x8_raw[:].rearrange("p j (q m) -> p q j m", m=DT)[:, q0:q1, :, 2 * s : 2 * s + 2],
             )
 
-        interleave_x8(nc.scalar.copy, 1)
-        interleave_x8(nc.scalar.copy, 2)
-        interleave_x8(nc.vector.tensor_copy, 0)
-        interleave_x8(nc.vector.tensor_copy, 3)
+        for a in range(2):
+            interleave(nc.scalar.copy, dy_grouped[a], dy_raw[a], NT, H)
+        interleave(nc.scalar.copy, dy_grouped[2], dy_raw[2], 576, H)
+
+        def quantize_dy(a, w0, w1):
+            quantize(dy_codes[a], dy_plane[a], dy_grouped[a], E5M2, w0, w1)
+
+        def multiply_early(a, h):
+            for u in range(h, BANKS, HT):
+                multiply(a, u)
+
+        half = NT // 2
+        interleave(nc.vector.tensor_copy, dy_grouped[0], dy_raw[0], 0, half)
+        interleave(nc.vector.tensor_copy, dy_grouped[0], dy_raw[0], half, NT)
+        quantize_dy(0, 0, half)
+        quantize_dy(0, half, NT)
+        multiply_early(0, 0)
+        interleave(nc.vector.tensor_copy, dy_grouped[1], dy_raw[1], 0, NT)
+        quantize_dy(0, NT, H)
+        multiply_early(0, 1)
+        quantize_dy(1, 0, NT)
+        multiply_early(1, 0)
+        interleave(nc.vector.tensor_copy, dy_grouped[2], dy_raw[2], 0, 576)
+        quantize_dy(1, NT, H)
+        multiply_early(1, 1)
+        quantize_dy(2, 0, NT)
+        quantize_dy(2, NT, H)
+
+        interleave_x8(nc.scalar.copy, 0, 88, 128)
+        interleave_x8(nc.scalar.copy, 1, 88, 128)
+        interleave_x8(nc.scalar.copy, 2, 40, 84)
+        interleave_x8(nc.vector.tensor_copy, 0, 0, 88)
+        interleave_x8(nc.vector.tensor_copy, 1, 0, 44)
         quantize_x8(0, 1)
         quantize_x8(1, 2)
-        interleave_x8(nc.vector.tensor_copy, 4)
+        interleave_x8(nc.vector.tensor_copy, 1, 44, 88)
+        interleave_x8(nc.vector.tensor_copy, 2, 0, 40)
         quantize_x8(2, 4)
-        quantize_x8(4, 5)
-        for m in range(early):
-            for h in range(HT):
-                multiply(2, m, h)
-        finish_on_scalar_and_gpsimd(0, 0)
-        interleave_x8(nc.scalar.copy, 5)
-        finish(0, 1)
-        finish(1, 0)
-        finish(1, 1)
-        store_pair(0)
-        quantize_x8(5, 6)
-        finish_on_scalar_and_gpsimd(2, 0)
-        for m in range(early, DT):
-            for h in range(HT):
-                for a in range(3):
-                    multiply(a, m, h)
-        finish(2, 1)
-        finish(3, 0)
-        finish(3, 1)
-        store_pair(1)
-        finish_on_scalar_and_gpsimd(4, 0)
-        finish(4, 1)
-        finish(5, 0)
-        finish(5, 1)
-        store_pair(2)
+        for u in range(BANKS):
+            multiply(2, u)
+        drain(0, 512)
+        decay_and_add(0, 320)
+        finish(704, 1024)
+        drain(512, 704)
+        decay_and_add(320, 704)
+        finish(1024, 1536)
+        finish(1536, 1792)
+        finish(1792, 2048)
+        finish(2048, 2560)
+        finish(2560, 3072)
+        store(0, 3072)
+        interleave_x8(nc.scalar.copy, 2, 84, 128)
+        drain(3072, 3584)
+        drain(3584, 3776)
+        quantize_x8(4, 6)
+        for u in (8, 9, 10):
+            multiply(0, u)
+            multiply(1, u)
+        multiply(2, 8)
+        multiply(2, 9)
+        multiply(0, 11)
+        multiply(1, 11)
+        multiply(2, 10)
+        multiply(2, 11)
+        decay_and_add(3072, 3392)
+        decay_and_add(3392, 3776)
+        finish(3776, 4096)
+        finish(4096, 4608)
+        finish(4608, 4992)
+        finish(4992, 5120)
+        finish(5120, 5632)
+        finish(5632, WIDTH)
+        store(3072, WIDTH)

@@ -77,7 +77,7 @@ def tile_mix_dwsav_ema_kernel(tc, x4_words, x4_scales, x8, dy, mom, out):
         nc.sync.dma_start(out=x8_raw[:], in_=x8.rearrange("(p j) d -> p j d", j=PACK))
         mom_rows = mom.rearrange("(p m) h -> p (m h)", m=DT)
         out_rows = out.rearrange("(p m) h -> p (m h)", m=DT)
-        load_cuts = [0, 1792, 3072, 4992, WIDTH]
+        load_cuts = [0, 2048, 4096, WIDTH]
         for c0, c1 in zip(load_cuts, load_cuts[1:]):
             nc.sync.dma_start(out=mom_sb[:, c0:c1], in_=mom_rows[:, c0:c1])
 
@@ -107,7 +107,7 @@ def tile_mix_dwsav_ema_kernel(tc, x4_words, x4_scales, x8, dy, mom, out):
             return x8_codes[:, cols].bitcast(E4M3), x8_plane[:, cols]
 
         acc = {}
-        bank_of = [0, 1, 2, 3, 4, 5, 6, 7, 0, 1, 2, 3]
+        bank_of = [0, 1, 2, 3, 4, 5, 6, 7, 1, 2, 3, 0]
 
         def multiply(a, u):
             m, h = divmod(u, HT)
@@ -193,36 +193,23 @@ def tile_mix_dwsav_ema_kernel(tc, x4_words, x4_scales, x8, dy, mom, out):
         quantize_x8(2, 4)
         for u in range(BANKS):
             multiply(2, u)
-        drain(0, 512)
-        decay_and_add(0, 320)
-        finish(704, 1024)
-        drain(512, 704)
-        decay_and_add(320, 704)
-        finish(1024, 1536)
-        finish(1536, 1792)
-        finish(1792, 2048)
-        finish(2048, 2560)
-        finish(2560, 3072)
-        store(0, 3072)
+        def finish_third(c0):
+            decay_and_add(c0, c0 + 448)
+            for u in range(c0 // NT + 1, c0 // NT + 4):
+                finish(NT * u, NT * (u + 1))
+            finish(c0 + 448, c0 + NT)
+            store(c0, c0 + 2048)
+
+        drain(0, 448)
+        finish_third(0)
+        drain(2048, 2496)
         interleave_x8(nc.scalar.copy, 2, 84, 128)
-        drain(3072, 3584)
-        drain(3584, 3776)
         quantize_x8(4, 6)
-        for u in (8, 9, 10):
-            multiply(0, u)
-            multiply(1, u)
-        multiply(2, 8)
-        multiply(2, 9)
-        multiply(0, 11)
-        multiply(1, 11)
-        multiply(2, 10)
-        multiply(2, 11)
-        decay_and_add(3072, 3392)
-        decay_and_add(3392, 3776)
-        finish(3776, 4096)
-        finish(4096, 4608)
-        finish(4608, 4992)
-        finish(4992, 5120)
-        finish(5120, 5632)
-        finish(5632, WIDTH)
-        store(3072, WIDTH)
+        finish_third(2048)
+        for u in range(BANKS, 12):
+            for a in range(2):
+                multiply(a, u)
+        for u in range(BANKS, 12):
+            multiply(2, u)
+        drain(4096, 4544)
+        finish_third(4096)

@@ -65,13 +65,14 @@ def tile_mix_dwsav_ema_kernel(tc, x4_words, x4_scales, x8, dy, mom, out):
         nc.gpsimd.memset(x4_plane_raw[:].rearrange("p a n -> p (a n)").bitcast(I32), 0)
 
         nc.sync.dma_start(out=x4_codes_raw[:].bitcast(I32), in_=x4_words.rearrange("a p n -> p a n").bitcast(I32))
-        for r in range(3):
-            (nc.scalar if r < 2 else nc.sync).dma_start(
-                out=x4_rows[r:P:32, :, :].bitcast(I32),
-                in_=x4_scales[:, r:16:4, :].rearrange("a q n -> q a n").bitcast(I32),
+        for q in (2, 3):
+            nc.scalar.dma_start(
+                out=x4_rows[32 * q : 32 * q + 4, :, :].bitcast(I32),
+                in_=x4_scales[:, 4 * q : 4 * q + 4, :].rearrange("a r n -> r a n").bitcast(I32),
             )
+        nc.sync.dma_start(out=x4_rows[0:4, :, :].bitcast(I32), in_=x4_scales[:, 0:4, :].rearrange("a r n -> r a n").bitcast(I32))
         for a in range(2):
-            nc.sync.dma_start(out=x4_rows[3:P:32, a, :].bitcast(I32), in_=x4_scales[a, 3:16:4, :].bitcast(I32))
+            nc.sync.dma_start(out=x4_rows[32:36, a, :].bitcast(I32), in_=x4_scales[a, 4:8, :].bitcast(I32))
         nc.sync.dma_start(out=dy_raw4[:], in_=dy[:T4, :].rearrange("(a p j) h -> p a j h", a=2, j=PACK))
         nc.sync.dma_start(out=dy_raw8[:], in_=dy[T4:, :].rearrange("(p j) h -> p j h", j=PACK))
         nc.sync.dma_start(out=x8_raw[:], in_=x8.rearrange("(p j) d -> p j d", j=PACK))

from contextlib import ExitStack

import concourse.mybir as mybir

T4, T8, D, H = 1024, 512, 768, 1024
FLOPS = 2 * (T4 + T8) * D * H

F32 = mybir.dt.float32
BF16 = mybir.dt.bfloat16
I32 = mybir.dt.int32
U32 = mybir.dt.uint32
U8 = mybir.dt.uint8
E4M3 = mybir.dt.float8_e4m3fn_x4
E5M2 = mybir.dt.float8_e5m2_x4
E2M1 = mybir.dt.float4_e2m1fn_x4
MULT = mybir.AluOpType.mult
ADD = mybir.AluOpType.add
COPY = mybir.ActivationFunctionType.Copy

P = 128
PACK = 4
NT = 512
DT = D // P
HT = H // NT
BANKS = 8
WIDTH = DT * H


def interleave(copy, grouped, raw, w0, w1):
    copy(
        out=grouped[:, w0:w1, :].rearrange("p (c i) j -> p c j i", i=4),
        in_=raw[:, :, w0:w1].rearrange("p j (c i) -> p c j i", i=4),
    )


def tile_mix_dwsav_ema_kernel(tc, x4_words, x4_scales, x8, dy, mom, out):
    nc = tc.nc
    with ExitStack() as ctx:
        keep = ctx.enter_context(tc.tile_pool(name="keep", bufs=1))
        psum = ctx.enter_context(tc.psum_pool(name="psum", bufs=1))
        ctx.enter_context(tc.manual_schedule())

        x4_codes = keep.tile([P, 2, 2 * D], U8, align_bytes=256)
        x4_codes_raw = keep.tile([P, 2, 2 * D], U8, align_bytes=256)
        x4_rows = keep.tile([P, 2, D], U8, align_bytes=256)
        x4_plane_raw = keep.tile([P, 2, D], U8, align_bytes=256)
        x4_plane = keep.tile([P, 2, D], U8, align_bytes=256)
        x8_raw = keep.tile([P, PACK, D], F32, align_bytes=256)
        x8_grouped = keep.tile([P, D, PACK], BF16, align_bytes=256)
        x8_codes = keep.tile([P, D], U32, align_bytes=256)
        x8_plane = keep.tile([P, D], U8, align_bytes=256)
        mom_sb = keep.tile([P, WIDTH], F32, align_bytes=256)
        res = keep.tile([P, WIDTH], F32, align_bytes=256)
        sums = keep.tile([P, WIDTH], F32, align_bytes=256)
        decayed = keep.tile([P, WIDTH], F32, align_bytes=256)
        dy_raw4 = keep.tile([P, 2, PACK, H], F32, align_bytes=256)
        dy_raw8 = keep.tile([P, PACK, H], F32, align_bytes=256)
        dy_raw = [dy_raw4[:, 0], dy_raw4[:, 1], dy_raw8[:]]
        dy_grouped, dy_codes, dy_plane = [], [], []
        for a in range(3):
            dy_grouped.append(keep.tile([P, H, PACK], BF16, align_bytes=256, name="dy_grouped%d" % a))
            dy_codes.append(keep.tile([P, H], U32, align_bytes=256, name="dy_codes%d" % a))
            dy_plane.append(keep.tile([P, H], U8, align_bytes=256, name="dy_plane%d" % a))

        nc.gpsimd.memset(x4_plane_raw[:].rearrange("p a n -> p (a n)").bitcast(I32), 0)

        nc.sync.dma_start(out=x4_codes_raw[:].bitcast(I32), in_=x4_words.rearrange("a p n -> p a n").bitcast(I32))
        for q in (2, 3):
            nc.scalar.dma_start(
                out=x4_rows[32 * q : 32 * q + 4, :, :].bitcast(I32),
                in_=x4_scales[:, 4 * q : 4 * q + 4, :].rearrange("a r n -> r a n").bitcast(I32),
            )
        nc.sync.dma_start(out=x4_rows[0:4, :, :].bitcast(I32), in_=x4_scales[:, 0:4, :].rearrange("a r n -> r a n").bitcast(I32))
        for a in range(2):
            nc.sync.dma_start(out=x4_rows[32:36, a, :].bitcast(I32), in_=x4_scales[a, 4:8, :].bitcast(I32))
        nc.sync.dma_start(out=dy_raw4[:], in_=dy[:T4, :].rearrange("(a p j) h -> p a j h", a=2, j=PACK))
        nc.sync.dma_start(out=dy_raw8[:], in_=dy[T4:, :].rearrange("(p j) h -> p j h", j=PACK))
        nc.sync.dma_start(out=x8_raw[:], in_=x8.rearrange("(p j) d -> p j d", j=PACK))
        mom_rows = mom.rearrange("(p m) h -> p (m h)", m=DT)
        out_rows = out.rearrange("(p m) h -> p (m h)", m=DT)
        load_cuts = [0, 2048, 4096, WIDTH]
        for c0, c1 in zip(load_cuts, load_cuts[1:]):
            nc.sync.dma_start(out=mom_sb[:, c0:c1], in_=mom_rows[:, c0:c1])

        for a in range(2):
            nc.vector.tensor_copy(
                out=x4_codes[:, a, :].rearrange("p (m q b) -> p m q b", m=DT, b=2),
                in_=x4_codes_raw[:, a, :].rearrange("p (q m b) -> p m q b", m=DT, b=2),
            )
        for q in range(0, P, 32):
            nc.gpsimd.tensor_copy(out=x4_plane_raw[q : q + 4].bitcast(I32), in_=x4_rows[q : q + 4].bitcast(I32))
        nc.gpsimd.tensor_copy(
            out=x4_plane[:].rearrange("p a (m q) -> p a m q", m=DT),
            in_=x4_plane_raw[:].rearrange("p a (q m) -> p a m q", m=DT),
        )

        def quantize(codes, plane, grouped, fmt, w0, w1):
            nc.vector.quantize_mx(
                out=codes[:, w0:w1].bitcast(fmt),
                scales=plane[:, w0:w1],
                in_=grouped[:, w0:w1, :].rearrange("p w j -> p (w j)"),
            )

        def stationary(a, m):
            cols = slice(P * m, P * (m + 1))
            if a < 2:
                return x4_codes[:, a, 2 * P * m : 2 * P * (m + 1)].bitcast(E2M1), x4_plane[:, a, cols]
            return x8_codes[:, cols].bitcast(E4M3), x8_plane[:, cols]

        acc = {}
        bank_of = [0, 1, 2, 3, 4, 5, 6, 7, 1, 2, 3, 0]

        def multiply(a, u):
            m, h = divmod(u, HT)
            if a == 0:
                acc[u] = psum.tile([P, NT], F32, name="acc%d" % bank_of[u])
            codes, plane = stationary(a, m)
            cols = slice(NT * h, NT * (h + 1))
            nc.tensor.matmul_mx(
                out=acc[u][:],
                lhsT=codes,
                lhsT_scale=plane,
                rhs=dy_codes[a][:, cols].bitcast(E5M2),
                rhs_scale=dy_plane[a][:, cols],
                start=(a == 0),
                stop=(a == 2),
            )

        def in_bank(c0, c1):
            u = c0 // NT
            return acc[u][:, c0 - NT * u : c1 - NT * u]

        def finish(c0, c1):
            nc.vector.scalar_tensor_tensor(
                out=res[:, c0:c1], in0=mom_sb[:, c0:c1], scalar=0.9, in1=in_bank(c0, c1), op0=MULT, op1=ADD
            )

        def drain(c0, c1):
            nc.scalar.copy(out=sums[:, c0:c1], in_=in_bank(c0, c1))

        def decay_and_add(c0, c1):
            nc.scalar.activation(out=decayed[:, c0:c1], in_=mom_sb[:, c0:c1], func=COPY, scale=0.9)
            nc.gpsimd.tensor_tensor(out=res[:, c0:c1], in0=decayed[:, c0:c1], in1=sums[:, c0:c1], op=ADD)

        def store(c0, c1):
            nc.sync.dma_start(out=out_rows[:, c0:c1], in_=res[:, c0:c1])

        def quantize_x8(m0, m1):
            quantize(x8_codes, x8_plane, x8_grouped, E4M3, P * m0, P * m1)

        def interleave_x8(copy, s, q0, q1):
            copy(
                out=x8_grouped[:].rearrange("p (m q) j -> p q j m", m=DT)[:, q0:q1, :, 2 * s : 2 * s + 2],
                in_=x8_raw[:].rearrange("p j (q m) -> p q j m", m=DT)[:, q0:q1, :, 2 * s : 2 * s + 2],
            )

        for a in range(2):
            interleave(nc.scalar.copy, dy_grouped[a], dy_raw[a], NT, H)
        interleave(nc.scalar.copy, dy_grouped[2], dy_raw[2], 576, H)

        def quantize_dy(a, w0, w1):
            quantize(dy_codes[a], dy_plane[a], dy_grouped[a], E5M2, w0, w1)

        def multiply_early(a, h):
            for u in range(h, BANKS, HT):
                multiply(a, u)

        half = NT // 2
        interleave(nc.vector.tensor_copy, dy_grouped[0], dy_raw[0], 0, half)
        interleave(nc.vector.tensor_copy, dy_grouped[0], dy_raw[0], half, NT)
        quantize_dy(0, 0, half)
        quantize_dy(0, half, NT)
        multiply_early(0, 0)
        interleave(nc.vector.tensor_copy, dy_grouped[1], dy_raw[1], 0, NT)
        quantize_dy(0, NT, H)
        multiply_early(0, 1)
        quantize_dy(1, 0, NT)
        multiply_early(1, 0)
        interleave(nc.vector.tensor_copy, dy_grouped[2], dy_raw[2], 0, 576)
        quantize_dy(1, NT, H)
        multiply_early(1, 1)
        quantize_dy(2, 0, NT)
        quantize_dy(2, NT, H)

        interleave_x8(nc.scalar.copy, 0, 88, 128)
        interleave_x8(nc.scalar.copy, 1, 88, 128)
        interleave_x8(nc.scalar.copy, 2, 40, 84)
        interleave_x8(nc.vector.tensor_copy, 0, 0, 88)
        interleave_x8(nc.vector.tensor_copy, 1, 0, 44)
        quantize_x8(0, 1)
        quantize_x8(1, 2)
        interleave_x8(nc.vector.tensor_copy, 1, 44, 88)
        interleave_x8(nc.vector.tensor_copy, 2, 0, 40)
        quantize_x8(2, 4)
        for u in range(BANKS):
            multiply(2, u)
        def finish_third(c0):
            decay_and_add(c0, c0 + 448)
            for u in range(c0 // NT + 1, c0 // NT + 4):
                finish(NT * u, NT * (u + 1))
            finish(c0 + 448, c0 + NT)
            store(c0, c0 + 2048)

        drain(0, 448)
        finish_third(0)
        drain(2048, 2496)
        interleave_x8(nc.scalar.copy, 2, 84, 128)
        quantize_x8(4, 6)
        finish_third(2048)
        for u in range(BANKS, 12):
            for a in range(2):
                multiply(a, u)
        for u in range(BANKS, 12):
            multiply(2, u)
        drain(4096, 4544)
        finish_third(4096)
